import numpy as np
import ml_dtypes


def mxq(x, axis, fmt="e4m3"):
    dtype, down = {"e4m3": (ml_dtypes.float8_e4m3fn, 7), "e5m2": (ml_dtypes.float8_e5m2, 14)}[fmt]
    v = np.moveaxis(np.asarray(x, np.float32).astype(ml_dtypes.bfloat16).astype(np.float64), axis, -1)
    blocks = v.reshape(v.shape[:-1] + (-1, 32))
    amax = np.abs(blocks).max(-1, keepdims=True)
    byte = np.maximum(np.where(amax > 0, np.frexp(amax)[1] - 1 + 127, 0) - down, 1)
    scale = np.exp2(byte - 127.0)
    codes = (blocks / scale).astype(np.float32).astype(dtype).astype(np.float64)
    return np.moveaxis((codes * scale).reshape(v.shape), -1, axis)


WIDE = False


def mx_kscale(k):
    if not WIDE:
        return np.ones(k)
    levels = np.array([10, -10, 5, -5, 0])
    if k % 512:
        return np.exp2(np.random.permutation(np.resize(levels, k // 32))).repeat(32)
    a = np.empty((k // 512, 16))
    for p in range(k // 512):
        a[p, :8] = np.random.permutation(np.resize(levels, 8))
        for g in range(8):
            far = levels[np.abs(levels - a[p, g]) >= 10]
            a[p, g + 8] = far[np.random.randint(len(far))]
    return np.exp2(a.ravel()).repeat(32)


def f64(x):
    return np.asarray(x).astype(np.float64)


def striped(idx):
    return np.tile(np.asarray(idx).reshape(-1, 16).T, (8, 1)).astype(np.uint16)


def unstriped(offs):
    return offs[:16].T.reshape(-1).astype(np.int64)


E2M1 = np.array([0.0, 0.5, 1.0, 1.5, 2.0, 3.0, 4.0, 6.0, -0.0, -0.5, -1.0, -1.5, -2.0, -3.0, -4.0, -6.0])


def pack_weight(w, fmt):
    k, n = w.shape
    w = f64(np.asarray(w, np.float32).astype(ml_dtypes.bfloat16)).reshape(k // 32, 32, n)
    amax = np.abs(w).max(1)
    if fmt == "e4m3":
        byte = np.frexp(amax)[1] - 1 + 127 - 7
    else:
        mant, ex = np.frexp(amax / 6.0)
        byte = np.where(mant > 0.5, ex, ex - 1) + 127
    byte = np.clip(np.where(amax > 0, byte, 1), 1, 254)
    scaled = (w * np.exp2(127.0 - byte)[:, None, :]).reshape(k, n).astype(np.float32)
    by_word = np.ascontiguousarray(scaled.reshape(k // 512, 128, 4, n).transpose(0, 1, 3, 2))
    if fmt == "e4m3":
        words = by_word.astype(ml_dtypes.float8_e4m3fn).view(np.uint8)
    else:
        c = by_word.astype(ml_dtypes.float4_e2m1fn).view(np.uint8) & 0xF
        words = (c[..., 0::2] | (c[..., 1::2] << 4)).reshape(k // 512, 128, 2 * n)
    return np.ascontiguousarray(words), np.ascontiguousarray(byte.astype(np.uint8).reshape(k // 512, 16, n))


def unpack_weight(words, scales, fmt):
    g, _, n = scales.shape
    words = np.ascontiguousarray(words).reshape(g, 128, n, -1)
    if fmt == "e4m3":
        vals = words.view(ml_dtypes.float8_e4m3fn).astype(np.float64)
    else:
        nib = np.empty((g, 128, n, 4), np.uint8)
        nib[..., 0::2] = words & 0xF
        nib[..., 1::2] = words >> 4
        vals = E2M1[nib]
    vals = vals * np.repeat(np.exp2(scales.astype(np.float64) - 127.0), 8, axis=1)[..., None]
    return vals.transpose(0, 1, 3, 2).reshape(g * 512, n)


D, T, I, J, U, E, M, C = 512, 2048, 512, 256, 1024, 512, 1024, 512


def setup_inputs():
    n = np.random.standard_normal
    idx = np.random.permutation(T)[:I]
    idx2 = np.random.permutation(U)[:J]
    idx3 = np.random.permutation(M)[:J]
    fd = mx_kscale(D)
    fi = mx_kscale(I)
    fc = mx_kscale(C)
    ti = np.ones(T)
    ti[idx] = fi
    keysp = pack_weight(n((D, T)) / fd[:, None], "e4m3")
    return {
        "keys_words": keysp[0],
        "keys_scales": keysp[1],
        "notes": (n((D, U)) * 1.0 / np.sqrt(D) * fd[:, None]).astype(np.float32),
        "rowf": (np.random.uniform(0.02, 0.08, (I, 1)) * fi[:, None]).astype(np.float32),
        "vals": (n((E, T)) / ti).astype(np.float32),
        "wm": (n((C, E)) * 1.0 / np.sqrt(C) * fc[:, None]).astype(np.float32),
        "mstore": (n((C, M)) / fc[:, None]).astype(np.float32),
        "offs": striped(idx),
        "offs2": striped(idx2),
        "offs3": striped(idx3),
    }


def reference(keys_words, keys_scales, notes, rowf, vals, wm, mstore, offs, offs2, offs3):
    idx = unstriped(offs)
    idx2 = unstriped(offs2)
    idx3 = unstriped(offs3)
    keysu = unpack_weight(keys_words, keys_scales, "e4m3")
    keysidxg = keysu[:, idx]
    notesidx2q = mxq(f64(notes)[:, idx2], 0, "e4m3")
    g9 = keysidxg.T @ notesidx2q
    g0 = np.maximum(g9, 0.0)
    gr1 = g0 * f64(rowf)
    vt1 = f64(vals)[:, idx].T
    vt1q = mxq(vt1, 0, "e4m3")
    gr1q = mxq(gr1, 0, "e4m3")
    o = vt1q.T @ gr1q
    wmq = mxq(f64(wm), 0, "e4m3")
    mstoreq = mxq(f64(mstore), 0, "e4m3")
    me = wmq.T @ mstoreq
    y = o * me[:, idx3]
    return y

@@ -1,0 +1,159 @@
+from contextlib import ExitStack
+
+import concourse.mybir as mybir
+from concourse.masks import make_identity
+
+D, T, I, J, U, E, M, C = 512, 2048, 512, 256, 1024, 512, 1024, 512
+FLOPS = 2 * (D * I * J + I * E * J + C * E * M)
+
+F32 = mybir.dt.float32
+BF16 = mybir.dt.bfloat16
+I32 = mybir.dt.int32
+U32 = mybir.dt.uint32
+U16 = mybir.dt.uint16
+U8 = mybir.dt.uint8
+FP8X4 = mybir.dt.float8_e4m3fn_x4
+COPY = mybir.ActivationFunctionType.Copy
+MULT = mybir.AluOpType.mult
+MAX = mybir.AluOpType.max
+
+P = 128
+PACK = 4
+BANK = 512
+E_TILES = E // P
+
+
+def tile_attend_tab_plain_gains_kernel(tc, keys_words, keys_scales, notes, rowf, vals, wm, mstore, offs, offs2, offs3, out):
+    nc = tc.nc
+    with ExitStack() as ctx:
+        sb = ctx.enter_context(tc.tile_pool(name="sb", bufs=1))
+        ps1 = ctx.enter_context(tc.psum_pool(name="ps1", bufs=1))
+        ps2 = ctx.enter_context(tc.psum_pool(name="ps2", bufs=2))
+
+        def tile(name, shape, dtype):
+            return sb.tile(shape, dtype, name=name, align_bytes=64)
+
+        def quantize(name, grouped):
+            width = grouped.shape[1] // PACK
+            codes = tile(name + "_codes", [P, width], U32)
+            scales = tile(name + "_scales", [P, width], U8)
+            nc.vector.quantize_mx(out=codes[:].bitcast(FP8X4), scales=scales[:], in_=grouped)
+            return codes, scales
+
+        def interleave(name, raw):
+            width = raw.shape[2]
+            grouped = tile(name + "_bf16", [P, width * PACK], BF16)
+            nc.vector.tensor_copy(
+                out=grouped[:].rearrange("p (c i t) -> p c t i", i=4, t=PACK),
+                in_=raw[:].rearrange("p t (c i) -> p c t i", i=4),
+            )
+            return grouped
+
+        def product(acc, lhs, lhs_cols, rhs, rhs_cols):
+            nc.tensor.matmul_mx(
+                out=acc,
+                lhsT=lhs[0][:, lhs_cols].bitcast(FP8X4),
+                lhsT_scale=lhs[1][:, lhs_cols],
+                rhs=rhs[0][:, rhs_cols].bitcast(FP8X4),
+                rhs_scale=rhs[1][:, rhs_cols],
+                start=True,
+                stop=True,
+            )
+
+        key_bytes = tile("key_bytes", [P, T], U8)
+        nc.vector.memset(key_bytes[:].bitcast(I32), 0)
+        identity = tile("identity", [P, P], F32)
+        make_identity(nc, identity[:])
+
+        wm_raw = tile("wm_raw", [P, PACK, E], F32)
+        ms_raw = [tile("ms_raw%d" % h, [P, PACK, BANK], F32) for h in range(M // BANK)]
+        key_words = tile("key_words", [P, T], I32)
+        note_planes = [tile("note_plane%d" % t, [P, U], F32) for t in range(PACK)]
+        val_rows = [tile("val_rows%d" % a, [P, T], F32) for a in range(E_TILES)]
+        list1 = tile("list1", [P, I // 16], U16)
+        list2 = tile("list2", [P, J // 16], U16)
+        list3 = tile("list3", [P, J // 16], U16)
+        row_factor = tile("row_factor", [P, PACK], F32)
+
+        ms_view = mstore.rearrange("(p t) m -> p t m", t=PACK)
+        notes_view = notes.rearrange("(p t) u -> p t u", t=PACK)
+        nc.sync.dma_start(out=wm_raw[:], in_=wm.rearrange("(p t) e -> p t e", t=PACK))
+        nc.sync.dma_start(list1[:], offs)
+        nc.sync.dma_start(out=ms_raw[0][:], in_=ms_view[:, :, 0:BANK])
+        nc.sync.dma_start(list2[:], offs2)
+        nc.sync.dma_start(out=ms_raw[1][:], in_=ms_view[:, :, BANK : 2 * BANK])
+        nc.sync.dma_start(list3[:], offs3)
+        nc.sync.dma_start(out=key_words[:], in_=keys_words[0].rearrange("p n r -> p (n r)").bitcast(I32))
+        nc.sync.dma_start(out=row_factor[:], in_=rowf.rearrange("(p t) o -> p (t o)", t=PACK))
+        for t in range(PACK):
+            nc.sync.dma_start(
+                out=key_bytes[32 * t : 32 * t + 4, :].bitcast(I32),
+                in_=keys_scales[0, 4 * t : 4 * t + 4, :].bitcast(I32),
+            )
+            nc.sync.dma_start(out=note_planes[t][:], in_=notes_view[:, t, :])
+        for a in range(E_TILES):
+            nc.sync.dma_start(out=val_rows[a][:], in_=vals[a * P : (a + 1) * P, :])
+
+        wm_q = quantize("wm", interleave("wm", wm_raw)[:])
+        me = [tile("me%d" % a, [P, M], F32) for a in range(E_TILES)]
+        for h in range(M // BANK):
+            ms_q = quantize("ms%d" % h, interleave("ms%d" % h, ms_raw[h])[:])
+            for a in range(E_TILES):
+                acc = ps2.tile([P, BANK], F32, name="me_bank")
+                product(acc[:], wm_q, slice(a * P, (a + 1) * P), ms_q, slice(0, BANK))
+                nc.scalar.copy(out=me[a][:, h * BANK : (h + 1) * BANK], in_=acc[:])
+
+        picked_words = tile("picked_words", [P, I], U32)
+        picked_bytes = tile("picked_bytes", [P, I], U8)
+        nc.vector.tensor_copy(
+            out=picked_words[:].rearrange("p (r s) -> p s r", r=PACK),
+            in_=key_words[:].bitcast(U32).indirect(list1[:]),
+        )
+        nc.vector.tensor_copy(
+            out=picked_bytes[:].rearrange("p (r s) -> p s r", r=PACK),
+            in_=key_bytes[:].indirect(list1[:]),
+        )
+
+        picked_notes = tile("picked_notes", [P, PACK, J], F32)
+        for t in range(PACK):
+            nc.scalar.activation(picked_notes[:, t, :], note_planes[t][:].indirect(list2[:]), COPY)
+        picked_me = [tile("picked_me%d" % a, [P, J], F32) for a in range(E_TILES)]
+        for a in range(E_TILES):
+            nc.scalar.activation(picked_me[a][:], me[a][:].indirect(list3[:]), COPY)
+        notes_q = quantize("notes", interleave("notes", picked_notes)[:])
+
+        table = tile("table_bf16", [P, J * PACK], BF16)
+        for h in range(J // P):
+            acc = ps1.tile([P, PACK, P], F32, name="table_bank%d" % h)
+            for r in range(PACK):
+                product(acc[:, r, :], (picked_words, picked_bytes), slice(r * P, (r + 1) * P), notes_q, slice(h * P, (h + 1) * P))
+            nc.vector.scalar_tensor_tensor(
+                out=table[:, h * BANK : (h + 1) * BANK].rearrange("p (j r) -> p j r", r=PACK),
+                in0=acc[:].rearrange("p r j -> p j r"),
+                scalar=0.0,
+                in1=row_factor[:].unsqueeze(1).to_broadcast([P, P, PACK]),
+                op0=MAX,
+                op1=MULT,
+            )
+        table_q = quantize("table", table[:])
+
+        half = I // 2
+        for a in range(E_TILES):
+            picked_vals = tile("picked_vals%d" % a, [P, I], BF16)
+            nc.vector.tensor_copy(out=picked_vals[:, 0:half], in_=val_rows[a][:].indirect(list1[:, 0 : half // 16]))
+            nc.scalar.activation(picked_vals[:, half:I], val_rows[a][:].indirect(list1[:, half // 16 : I // 16]), COPY)
+            pairs = picked_vals[:].bitcast(F32)
+            turned = ps2.tile([P, 2, P], F32, name="turn_bank")
+            for u in range(2):
+                nc.tensor.transpose(turned[:, u, :], pairs[:, u : I // 2 : 2], identity[:])
+            grouped = tile("vals%d_bf16" % a, [P, P * PACK], BF16)
+            nc.scalar.copy(
+                out=grouped[:].bitcast(F32).rearrange("p (e u) -> p e u", u=2),
+                in_=turned[:].rearrange("p u e -> p e u"),
+            )
+            vals_q = quantize("vals%d" % a, grouped[:])
+            acc = ps2.tile([P, J], F32, name="out_bank")
+            product(acc[:], vals_q, slice(0, P), table_q, slice(0, J))
+            result = tile("result%d" % a, [P, J], F32)
+            nc.vector.tensor_tensor(result[:], acc[:], picked_me[a][:], MULT)
+            nc.sync.dma_start(out=out[a * P : (a + 1) * P, :], in_=result[:])

@@ -30,12 +30,12 @@ def tile_attend_tab_plain_gains_kernel(tc, keys_words, keys_scales, notes, rowf,
         ps1 = ctx.enter_context(tc.psum_pool(name="ps1", bufs=1))
         ps2 = ctx.enter_context(tc.psum_pool(name="ps2", bufs=2))
 
-        def tile(name, shape, dtype):
-            return sb.tile(shape, dtype, name=name, align_bytes=64)
+        def tile(name, shape, dtype, buffer=None):
+            return sb.tile(shape, dtype, name=name, tag=buffer or name, align_bytes=64)
 
-        def quantize(name, grouped):
+        def quantize(name, grouped, buffer=None):
             width = grouped.shape[1] // PACK
-            codes = tile(name + "_codes", [P, width], U32)
+            codes = tile(name + "_codes", [P, width], U32, buffer)
             scales = tile(name + "_scales", [P, width], U8)
             nc.vector.quantize_mx(out=codes[:].bitcast(FP8X4), scales=scales[:], in_=grouped)
             return codes, scales
@@ -61,7 +61,7 @@ def tile_attend_tab_plain_gains_kernel(tc, keys_words, keys_scales, notes, rowf,
             )
 
         key_bytes = tile("key_bytes", [P, T], U8)
-        nc.vector.memset(key_bytes[:].bitcast(I32), 0)
+        nc.gpsimd.memset(key_bytes[:].bitcast(I32), 0)
         identity = tile("identity", [P, P], F32)
         make_identity(nc, identity[:])
 
@@ -79,18 +79,19 @@ def tile_attend_tab_plain_gains_kernel(tc, keys_words, keys_scales, notes, rowf,
         notes_view = notes.rearrange("(p t) u -> p t u", t=PACK)
         nc.sync.dma_start(out=wm_raw[:], in_=wm.rearrange("(p t) e -> p t e", t=PACK))
         nc.sync.dma_start(list1[:], offs)
-        nc.sync.dma_start(out=ms_raw[0][:], in_=ms_view[:, :, 0:BANK])
-        nc.sync.dma_start(list2[:], offs2)
-        nc.sync.dma_start(out=ms_raw[1][:], in_=ms_view[:, :, BANK : 2 * BANK])
-        nc.sync.dma_start(list3[:], offs3)
-        nc.sync.dma_start(out=key_words[:], in_=keys_words[0].rearrange("p n r -> p (n r)").bitcast(I32))
-        nc.sync.dma_start(out=row_factor[:], in_=rowf.rearrange("(p t) o -> p (t o)", t=PACK))
-        for t in range(PACK):
+        for q in range(4):
             nc.sync.dma_start(
-                out=key_bytes[32 * t : 32 * t + 4, :].bitcast(I32),
-                in_=keys_scales[0, 4 * t : 4 * t + 4, :].bitcast(I32),
+                out=key_bytes[32 * q : 32 * q + 4, :].bitcast(I32),
+                in_=keys_scales[0, 4 * q : 4 * q + 4, :].bitcast(I32),
             )
+        for h in range(M // BANK):
+            nc.sync.dma_start(out=ms_raw[h][:], in_=ms_view[:, :, h * BANK : (h + 1) * BANK])
+        nc.sync.dma_start(list2[:], offs2)
+        for t in range(PACK):
             nc.sync.dma_start(out=note_planes[t][:], in_=notes_view[:, t, :])
+        nc.sync.dma_start(list3[:], offs3)
+        nc.sync.dma_start(out=row_factor[:], in_=rowf.rearrange("(p t) o -> p (t o)", t=PACK))
+        nc.sync.dma_start(out=key_words[:], in_=keys_words[0].rearrange("p n r -> p (n r)").bitcast(I32))
         for a in range(E_TILES):
             nc.sync.dma_start(out=val_rows[a][:], in_=vals[a * P : (a + 1) * P, :])
 
@@ -116,7 +117,7 @@ def tile_attend_tab_plain_gains_kernel(tc, keys_words, keys_scales, notes, rowf,
 
         picked_notes = tile("picked_notes", [P, PACK, J], F32)
         for t in range(PACK):
-            nc.scalar.activation(picked_notes[:, t, :], note_planes[t][:].indirect(list2[:]), COPY)
+            nc.vector.tensor_copy(out=picked_notes[:, t, :], in_=note_planes[t][:].indirect(list2[:]))
         picked_me = [tile("picked_me%d" % a, [P, J], F32) for a in range(E_TILES)]
         for a in range(E_TILES):
             nc.scalar.activation(picked_me[a][:], me[a][:].indirect(list3[:]), COPY)
@@ -137,8 +138,11 @@ def tile_attend_tab_plain_gains_kernel(tc, keys_words, keys_scales, notes, rowf,
             )
         table_q = quantize("table", table[:])
 
-        half = I // 2
-        for a in range(E_TILES):
+        half = 320
+        grouped_vals = {}
+        sums = {}
+
+        def gather_and_turn(a):
             picked_vals = tile("picked_vals%d" % a, [P, I], BF16)
             nc.vector.tensor_copy(out=picked_vals[:, 0:half], in_=val_rows[a][:].indirect(list1[:, 0 : half // 16]))
             nc.scalar.activation(picked_vals[:, half:I], val_rows[a][:].indirect(list1[:, half // 16 : I // 16]), COPY)
@@ -151,9 +155,25 @@ def tile_attend_tab_plain_gains_kernel(tc, keys_words, keys_scales, notes, rowf,
                 out=grouped[:].bitcast(F32).rearrange("p (e u) -> p e u", u=2),
                 in_=turned[:].rearrange("p u e -> p e u"),
             )
-            vals_q = quantize("vals%d" % a, grouped[:])
+            grouped_vals[a] = grouped
+
+        def multiply(a):
+            buffer = "val_rows%d" % (a + 1) if a + 1 < E_TILES else None
+            vals_q = quantize("vals%d" % a, grouped_vals[a][:], buffer)
             acc = ps2.tile([P, J], F32, name="out_bank")
             product(acc[:], vals_q, slice(0, P), table_q, slice(0, J))
-            result = tile("result%d" % a, [P, J], F32)
-            nc.vector.tensor_tensor(result[:], acc[:], picked_me[a][:], MULT)
+            sums[a] = acc
+
+        def finish(a):
+            buffer = "vals%d_bf16" % (a + 1) if a + 1 < E_TILES else None
+            result = tile("result%d" % a, [P, J], F32, buffer)
+            nc.vector.tensor_tensor(result[:], sums[a][:], picked_me[a][:], MULT)
             nc.sync.dma_start(out=out[a * P : (a + 1) * P, :], in_=result[:])
+
+        for step in range(E_TILES + 2):
+            if step < E_TILES:
+                gather_and_turn(step)
+            if 1 <= step <= E_TILES:
+                multiply(step - 1)
+            if step >= 2:
+                finish(step - 2)

@@ -28,9 +28,11 @@ def tile_attend_tab_plain_gains_kernel(tc, keys_words, keys_scales, notes, rowf,
     with ExitStack() as ctx:
         sb = ctx.enter_context(tc.tile_pool(name="sb", bufs=1))
         ps1 = ctx.enter_context(tc.psum_pool(name="ps1", bufs=1))
-        ps2 = ctx.enter_context(tc.psum_pool(name="ps2", bufs=2))
+        rows = ctx.enter_context(tc.tile_pool(name="rows", bufs=1))
 
         def tile(name, shape, dtype, buffer=None):
+            if isinstance(buffer, int):
+                return rows.tile(shape, dtype, name=name, offset=buffer, align_bytes=64)
             return sb.tile(shape, dtype, name=name, tag=buffer or name, align_bytes=64)
 
         def quantize(name, grouped, buffer=None):
@@ -45,7 +47,7 @@ def tile_attend_tab_plain_gains_kernel(tc, keys_words, keys_scales, notes, rowf,
             grouped = tile(name + "_bf16", [P, width * PACK], BF16)
             nc.vector.tensor_copy(
                 out=grouped[:].rearrange("p (c i t) -> p c t i", i=4, t=PACK),
-                in_=raw[:].rearrange("p t (c i) -> p c t i", i=4),
+                in_=raw.rearrange("p t (c i) -> p c t i", i=4),
             )
             return grouped
 
@@ -68,62 +70,105 @@ def tile_attend_tab_plain_gains_kernel(tc, keys_words, keys_scales, notes, rowf,
         wm_raw = tile("wm_raw", [P, PACK, E], F32)
         ms_raw = [tile("ms_raw%d" % h, [P, PACK, BANK], F32) for h in range(M // BANK)]
         key_words = tile("key_words", [P, T], I32)
-        note_planes = [tile("note_plane%d" % t, [P, U], F32) for t in range(PACK)]
-        val_rows = [tile("val_rows%d" % a, [P, T], F32) for a in range(E_TILES)]
+        note_planes = [tile("note_planes%d" % v, [P, 2, U], F32) for v in range(PACK // 2)]
+        val_rows = [tile("val_rows%d" % a, [P, T], F32, a * 4 * T) for a in range(E_TILES)]
         list1 = tile("list1", [P, I // 16], U16)
         list2 = tile("list2", [P, J // 16], U16)
         list3 = tile("list3", [P, J // 16], U16)
         row_factor = tile("row_factor", [P, PACK], F32)
 
-        ms_view = mstore.rearrange("(p t) m -> p t m", t=PACK)
         notes_view = notes.rearrange("(p t) u -> p t u", t=PACK)
         nc.sync.dma_start(out=wm_raw[:], in_=wm.rearrange("(p t) e -> p t e", t=PACK))
         nc.sync.dma_start(list1[:], offs)
-        for q in range(4):
+        for r in range(4):
             nc.sync.dma_start(
-                out=key_bytes[32 * q : 32 * q + 4, :].bitcast(I32),
-                in_=keys_scales[0, 4 * q : 4 * q + 4, :].bitcast(I32),
+                out=key_bytes[r:P:32, :].bitcast(I32),
+                in_=keys_scales[0, r:16:4, :].bitcast(I32),
             )
+        ms_view = mstore.rearrange("(p t) m -> p t m", t=PACK)
+        nc.sync.dma_start(list2[:], offs2)
+        nc.sync.dma_start(out=note_planes[0][:], in_=notes_view[:, 0:2, :])
         for h in range(M // BANK):
             nc.sync.dma_start(out=ms_raw[h][:], in_=ms_view[:, :, h * BANK : (h + 1) * BANK])
-        nc.sync.dma_start(list2[:], offs2)
-        for t in range(PACK):
-            nc.sync.dma_start(out=note_planes[t][:], in_=notes_view[:, t, :])
+        nc.sync.dma_start(out=note_planes[1][:], in_=notes_view[:, 2:4, :])
         nc.sync.dma_start(list3[:], offs3)
         nc.sync.dma_start(out=row_factor[:], in_=rowf.rearrange("(p t) o -> p (t o)", t=PACK))
         nc.sync.dma_start(out=key_words[:], in_=keys_words[0].rearrange("p n r -> p (n r)").bitcast(I32))
         for a in range(E_TILES):
             nc.sync.dma_start(out=val_rows[a][:], in_=vals[a * P : (a + 1) * P, :])
 
-        wm_q = quantize("wm", interleave("wm", wm_raw)[:])
-        me = [tile("me%d" % a, [P, M], F32) for a in range(E_TILES)]
-        for h in range(M // BANK):
-            ms_q = quantize("ms%d" % h, interleave("ms%d" % h, ms_raw[h])[:])
-            for a in range(E_TILES):
-                acc = ps2.tile([P, BANK], F32, name="me_bank")
-                product(acc[:], wm_q, slice(a * P, (a + 1) * P), ms_q, slice(0, BANK))
-                nc.scalar.copy(out=me[a][:, h * BANK : (h + 1) * BANK], in_=acc[:])
-
-        picked_words = tile("picked_words", [P, I], U32)
         picked_bytes = tile("picked_bytes", [P, I], U8)
-        nc.vector.tensor_copy(
-            out=picked_words[:].rearrange("p (r s) -> p s r", r=PACK),
-            in_=key_words[:].bitcast(U32).indirect(list1[:]),
-        )
         nc.vector.tensor_copy(
             out=picked_bytes[:].rearrange("p (r s) -> p s r", r=PACK),
             in_=key_bytes[:].indirect(list1[:]),
         )
 
         picked_notes = tile("picked_notes", [P, PACK, J], F32)
-        for t in range(PACK):
-            nc.vector.tensor_copy(out=picked_notes[:, t, :], in_=note_planes[t][:].indirect(list2[:]))
-        picked_me = [tile("picked_me%d" % a, [P, J], F32) for a in range(E_TILES)]
-        for a in range(E_TILES):
-            nc.scalar.activation(picked_me[a][:], me[a][:].indirect(list3[:]), COPY)
-        notes_q = quantize("notes", interleave("notes", picked_notes)[:])
+        for t in range(2):
+            nc.scalar.activation(picked_notes[:, t, :], note_planes[0][:, t, :].indirect(list2[:]), COPY)
 
-        table = tile("table_bf16", [P, J * PACK], BF16)
+        wm_q = quantize("wm", interleave("wm", wm_raw[:])[:])
+        me = [tile("me%d" % a, [P, M], F32) for a in range(E_TILES)]
+        for h in range(M // BANK):
+            ms_q = quantize("ms%d" % h, interleave("ms%d" % h, ms_raw[h][:])[:])
+            for a in range(E_TILES):
+                acc = ps1.tile([P, BANK], F32, name="me_sums%d_%d" % (h, a), tag="value_bank%d" % a)
+                product(acc[:], wm_q, slice(a * P, (a + 1) * P), ms_q, slice(0, BANK))
+                nc.scalar.copy(out=me[a][:, h * BANK : (h + 1) * BANK], in_=acc[:])
+
+        picked_words = tile("picked_words", [P, I], U32)
+        nc.vector.tensor_copy(
+            out=picked_words[:].rearrange("p (r s) -> p s r", r=PACK),
+            in_=key_words[:].bitcast(U32).indirect(list1[:]),
+        )
+
+        for t in range(2):
+            nc.vector.tensor_copy(out=picked_notes[:, 2 + t, :], in_=note_planes[1][:, t, :].indirect(list2[:]))
+        picked_me = {}
+
+        def look_up(a):
+            picked_me[a] = tile("picked_me%d" % a, [P, J], F32, (a - 1) * 4 * T + 2 * T if a > 0 else None)
+            nc.scalar.activation(picked_me[a][:], me[a][:].indirect(list3[:]), COPY)
+
+        look_up(0)
+        notes_q = quantize("notes", interleave("notes", picked_notes[:])[:])
+
+        half = 288
+        grouped_vals = {}
+        sums = {}
+
+        def gather_and_turn(a):
+            picked_vals = tile("picked_vals%d" % a, [P, I], BF16)
+            nc.vector.tensor_copy(out=picked_vals[:, 0:half], in_=val_rows[a][:].indirect(list1[:, 0 : half // 16]))
+            nc.scalar.activation(picked_vals[:, half:I], val_rows[a][:].indirect(list1[:, half // 16 : I // 16]), COPY)
+            if a + 1 < E_TILES:
+                look_up(a + 1)
+            pairs = picked_vals[:].bitcast(F32)
+            turned = ps1.tile([P, 2, P], F32, name="turned%d" % a, tag="value_bank%d" % a)
+            for u in range(2):
+                nc.tensor.transpose(turned[:, u, :], pairs[:, u : I // 2 : 2], identity[:])
+            grouped = tile("vals%d_bf16" % a, [P, P * PACK], BF16)
+            nc.scalar.copy(
+                out=grouped[:].bitcast(F32).rearrange("p (e u) -> p e u", u=2),
+                in_=turned[:].rearrange("p u e -> p e u"),
+            )
+            grouped_vals[a] = grouped
+
+        def multiply(a):
+            buffer = (a + 1) * 4 * T if a + 1 < E_TILES else None
+            vals_q = quantize("vals%d" % a, grouped_vals[a][:], buffer)
+            acc = ps1.tile([P, J], F32, name="sums%d" % a, tag="value_bank%d" % ((a + 1) % E_TILES))
+            product(acc[:], vals_q, slice(0, P), table_q, slice(0, J))
+            sums[a] = acc
+
+        def finish(a):
+            buffer = "vals%d_bf16" % (a + 1) if a + 1 < E_TILES else None
+            result = tile("result%d" % a, [P, J], F32, buffer)
+            nc.vector.tensor_tensor(result[:], sums[a][:], picked_me[a][:], MULT)
+            nc.sync.dma_start(out=out[a * P : (a + 1) * P, :], in_=result[:])
+
+        gather_and_turn(0)
+        table = tile("table_bf16", [P, J * PACK], BF16, 0)
         for h in range(J // P):
             acc = ps1.tile([P, PACK, P], F32, name="table_bank%d" % h)
             for r in range(PACK):
@@ -138,42 +183,10 @@ def tile_attend_tab_plain_gains_kernel(tc, keys_words, keys_scales, notes, rowf,
             )
         table_q = quantize("table", table[:])
 
-        half = 320
-        grouped_vals = {}
-        sums = {}
-
-        def gather_and_turn(a):
-            picked_vals = tile("picked_vals%d" % a, [P, I], BF16)
-            nc.vector.tensor_copy(out=picked_vals[:, 0:half], in_=val_rows[a][:].indirect(list1[:, 0 : half // 16]))
-            nc.scalar.activation(picked_vals[:, half:I], val_rows[a][:].indirect(list1[:, half // 16 : I // 16]), COPY)
-            pairs = picked_vals[:].bitcast(F32)
-            turned = ps2.tile([P, 2, P], F32, name="turn_bank")
-            for u in range(2):
-                nc.tensor.transpose(turned[:, u, :], pairs[:, u : I // 2 : 2], identity[:])
-            grouped = tile("vals%d_bf16" % a, [P, P * PACK], BF16)
-            nc.scalar.copy(
-                out=grouped[:].bitcast(F32).rearrange("p (e u) -> p e u", u=2),
-                in_=turned[:].rearrange("p u e -> p e u"),
-            )
-            grouped_vals[a] = grouped
-
-        def multiply(a):
-            buffer = "val_rows%d" % (a + 1) if a + 1 < E_TILES else None
-            vals_q = quantize("vals%d" % a, grouped_vals[a][:], buffer)
-            acc = ps2.tile([P, J], F32, name="out_bank")
-            product(acc[:], vals_q, slice(0, P), table_q, slice(0, J))
-            sums[a] = acc
-
-        def finish(a):
-            buffer = "vals%d_bf16" % (a + 1) if a + 1 < E_TILES else None
-            result = tile("result%d" % a, [P, J], F32, buffer)
-            nc.vector.tensor_tensor(result[:], sums[a][:], picked_me[a][:], MULT)
-            nc.sync.dma_start(out=out[a * P : (a + 1) * P, :], in_=result[:])
-
-        for step in range(E_TILES + 2):
+        for step in range(1, E_TILES + 2):
             if step < E_TILES:
                 gather_and_turn(step)
-            if 1 <= step <= E_TILES:
+            if step <= E_TILES:
                 multiply(step - 1)
             if step >= 2:
                 finish(step - 2)

from contextlib import ExitStack

import concourse.mybir as mybir
from concourse.masks import make_identity

D, T, I, J, U, E, M, C = 512, 2048, 512, 256, 1024, 512, 1024, 512
FLOPS = 2 * (D * I * J + I * E * J + C * E * M)

F32 = mybir.dt.float32
BF16 = mybir.dt.bfloat16
I32 = mybir.dt.int32
U32 = mybir.dt.uint32
U16 = mybir.dt.uint16
U8 = mybir.dt.uint8
FP8X4 = mybir.dt.float8_e4m3fn_x4
COPY = mybir.ActivationFunctionType.Copy
MULT = mybir.AluOpType.mult
MAX = mybir.AluOpType.max

P = 128
PACK = 4
BANK = 512
E_TILES = E // P


def tile_attend_tab_plain_gains_kernel(tc, keys_words, keys_scales, notes, rowf, vals, wm, mstore, offs, offs2, offs3, out):
    nc = tc.nc
    with ExitStack() as ctx:
        sb = ctx.enter_context(tc.tile_pool(name="sb", bufs=1))
        ps1 = ctx.enter_context(tc.psum_pool(name="ps1", bufs=1))
        rows = ctx.enter_context(tc.tile_pool(name="rows", bufs=1))

        def tile(name, shape, dtype, buffer=None):
            if isinstance(buffer, int):
                return rows.tile(shape, dtype, name=name, offset=buffer, align_bytes=64)
            return sb.tile(shape, dtype, name=name, tag=buffer or name, align_bytes=64)

        def quantize(name, grouped, buffer=None):
            width = grouped.shape[1] // PACK
            codes = tile(name + "_codes", [P, width], U32, buffer)
            scales = tile(name + "_scales", [P, width], U8)
            nc.vector.quantize_mx(out=codes[:].bitcast(FP8X4), scales=scales[:], in_=grouped)
            return codes, scales

        def interleave(name, raw):
            width = raw.shape[2]
            grouped = tile(name + "_bf16", [P, width * PACK], BF16)
            nc.vector.tensor_copy(
                out=grouped[:].rearrange("p (c i t) -> p c t i", i=4, t=PACK),
                in_=raw.rearrange("p t (c i) -> p c t i", i=4),
            )
            return grouped

        def product(acc, lhs, lhs_cols, rhs, rhs_cols):
            nc.tensor.matmul_mx(
                out=acc,
                lhsT=lhs[0][:, lhs_cols].bitcast(FP8X4),
                lhsT_scale=lhs[1][:, lhs_cols],
                rhs=rhs[0][:, rhs_cols].bitcast(FP8X4),
                rhs_scale=rhs[1][:, rhs_cols],
                start=True,
                stop=True,
            )

        key_bytes = tile("key_bytes", [P, T], U8)
        nc.gpsimd.memset(key_bytes[:].bitcast(I32), 0)
        identity = tile("identity", [P, P], F32)
        make_identity(nc, identity[:])

        wm_raw = tile("wm_raw", [P, PACK, E], F32)
        ms_raw = [tile("ms_raw%d" % h, [P, PACK, BANK], F32) for h in range(M // BANK)]
        key_words = tile("key_words", [P, T], I32)
        note_planes = [tile("note_planes%d" % v, [P, 2, U], F32) for v in range(PACK // 2)]
        val_rows = [tile("val_rows%d" % a, [P, T], F32, a * 4 * T) for a in range(E_TILES)]
        list1 = tile("list1", [P, I // 16], U16)
        list2 = tile("list2", [P, J // 16], U16)
        list3 = tile("list3", [P, J // 16], U16)
        row_factor = tile("row_factor", [P, PACK], F32)

        notes_view = notes.rearrange("(p t) u -> p t u", t=PACK)
        nc.sync.dma_start(out=wm_raw[:], in_=wm.rearrange("(p t) e -> p t e", t=PACK))
        nc.sync.dma_start(list1[:], offs)
        for r in range(4):
            nc.sync.dma_start(
                out=key_bytes[r:P:32, :].bitcast(I32),
                in_=keys_scales[0, r:16:4, :].bitcast(I32),
            )
        ms_view = mstore.rearrange("(p t) m -> p t m", t=PACK)
        nc.sync.dma_start(list2[:], offs2)
        nc.sync.dma_start(out=note_planes[0][:], in_=notes_view[:, 0:2, :])
        for h in range(M // BANK):
            nc.sync.dma_start(out=ms_raw[h][:], in_=ms_view[:, :, h * BANK : (h + 1) * BANK])
        nc.sync.dma_start(out=note_planes[1][:], in_=notes_view[:, 2:4, :])
        nc.sync.dma_start(list3[:], offs3)
        nc.sync.dma_start(out=row_factor[:], in_=rowf.rearrange("(p t) o -> p (t o)", t=PACK))
        nc.sync.dma_start(out=key_words[:], in_=keys_words[0].rearrange("p n r -> p (n r)").bitcast(I32))
        for a in range(E_TILES):
            nc.sync.dma_start(out=val_rows[a][:], in_=vals[a * P : (a + 1) * P, :])

        picked_bytes = tile("picked_bytes", [P, I], U8)
        nc.vector.tensor_copy(
            out=picked_bytes[:].rearrange("p (r s) -> p s r", r=PACK),
            in_=key_bytes[:].indirect(list1[:]),
        )

        picked_notes = tile("picked_notes", [P, PACK, J], F32)
        for t in range(2):
            nc.scalar.activation(picked_notes[:, t, :], note_planes[0][:, t, :].indirect(list2[:]), COPY)

        wm_q = quantize("wm", interleave("wm", wm_raw[:])[:])
        me = [tile("me%d" % a, [P, M], F32) for a in range(E_TILES)]
        for h in range(M // BANK):
            ms_q = quantize("ms%d" % h, interleave("ms%d" % h, ms_raw[h][:])[:])
            for a in range(E_TILES):
                acc = ps1.tile([P, BANK], F32, name="me_sums%d_%d" % (h, a), tag="value_bank%d" % a)
                product(acc[:], wm_q, slice(a * P, (a + 1) * P), ms_q, slice(0, BANK))
                nc.scalar.copy(out=me[a][:, h * BANK : (h + 1) * BANK], in_=acc[:])

        picked_words = tile("picked_words", [P, I], U32)
        nc.vector.tensor_copy(
            out=picked_words[:].rearrange("p (r s) -> p s r", r=PACK),
            in_=key_words[:].bitcast(U32).indirect(list1[:]),
        )

        for t in range(2):
            nc.vector.tensor_copy(out=picked_notes[:, 2 + t, :], in_=note_planes[1][:, t, :].indirect(list2[:]))
        picked_me = {}

        def look_up(a):
            picked_me[a] = tile("picked_me%d" % a, [P, J], F32, (a - 1) * 4 * T + 2 * T if a > 0 else None)
            nc.scalar.activation(picked_me[a][:], me[a][:].indirect(list3[:]), COPY)

        look_up(0)
        notes_q = quantize("notes", interleave("notes", picked_notes[:])[:])

        half = 288
        grouped_vals = {}
        sums = {}

        def gather_and_turn(a):
            picked_vals = tile("picked_vals%d" % a, [P, I], BF16)
            nc.vector.tensor_copy(out=picked_vals[:, 0:half], in_=val_rows[a][:].indirect(list1[:, 0 : half // 16]))
            nc.scalar.activation(picked_vals[:, half:I], val_rows[a][:].indirect(list1[:, half // 16 : I // 16]), COPY)
            if a + 1 < E_TILES:
                look_up(a + 1)
            pairs = picked_vals[:].bitcast(F32)
            turned = ps1.tile([P, 2, P], F32, name="turned%d" % a, tag="value_bank%d" % a)
            for u in range(2):
                nc.tensor.transpose(turned[:, u, :], pairs[:, u : I // 2 : 2], identity[:])
            grouped = tile("vals%d_bf16" % a, [P, P * PACK], BF16)
            nc.scalar.copy(
                out=grouped[:].bitcast(F32).rearrange("p (e u) -> p e u", u=2),
                in_=turned[:].rearrange("p u e -> p e u"),
            )
            grouped_vals[a] = grouped

        def multiply(a):
            buffer = (a + 1) * 4 * T if a + 1 < E_TILES else None
            vals_q = quantize("vals%d" % a, grouped_vals[a][:], buffer)
            acc = ps1.tile([P, J], F32, name="sums%d" % a, tag="value_bank%d" % ((a + 1) % E_TILES))
            product(acc[:], vals_q, slice(0, P), table_q, slice(0, J))
            sums[a] = acc

        def finish(a):
            buffer = "vals%d_bf16" % (a + 1) if a + 1 < E_TILES else None
            result = tile("result%d" % a, [P, J], F32, buffer)
            nc.vector.tensor_tensor(result[:], sums[a][:], picked_me[a][:], MULT)
            nc.sync.dma_start(out=out[a * P : (a + 1) * P, :], in_=result[:])

        gather_and_turn(0)
        table = tile("table_bf16", [P, J * PACK], BF16, 0)
        for h in range(J // P):
            acc = ps1.tile([P, PACK, P], F32, name="table_bank%d" % h)
            for r in range(PACK):
                product(acc[:, r, :], (picked_words, picked_bytes), slice(r * P, (r + 1) * P), notes_q, slice(h * P, (h + 1) * P))
            nc.vector.scalar_tensor_tensor(
                out=table[:, h * BANK : (h + 1) * BANK].rearrange("p (j r) -> p j r", r=PACK),
                in0=acc[:].rearrange("p r j -> p j r"),
                scalar=0.0,
                in1=row_factor[:].unsqueeze(1).to_broadcast([P, P, PACK]),
                op0=MAX,
                op1=MULT,
            )
        table_q = quantize("table", table[:])

        for step in range(1, E_TILES + 2):
            if step < E_TILES:
                gather_and_turn(step)
            if step <= E_TILES:
                multiply(step - 1)
            if step >= 2:
                finish(step - 2)
